import numpy as np
import ml_dtypes


def mxq(x, axis, fmt="e4m3"):
    dtype, down = {"e4m3": (ml_dtypes.float8_e4m3fn, 7), "e5m2": (ml_dtypes.float8_e5m2, 14)}[fmt]
    v = np.moveaxis(np.asarray(x, np.float32).astype(ml_dtypes.bfloat16).astype(np.float64), axis, -1)
    blocks = v.reshape(v.shape[:-1] + (-1, 32))
    amax = np.abs(blocks).max(-1, keepdims=True)
    byte = np.maximum(np.where(amax > 0, np.frexp(amax)[1] - 1 + 127, 0) - down, 1)
    scale = np.exp2(byte - 127.0)
    codes = (blocks / scale).astype(np.float32).astype(dtype).astype(np.float64)
    return np.moveaxis((codes * scale).reshape(v.shape), -1, axis)


WIDE = False


def mx_kscale(k):
    if not WIDE:
        return np.ones(k)
    levels = np.array([10, -10, 5, -5, 0])
    if k % 512:
        return np.exp2(np.random.permutation(np.resize(levels, k // 32))).repeat(32)
    a = np.empty((k // 512, 16))
    for p in range(k // 512):
        a[p, :8] = np.random.permutation(np.resize(levels, 8))
        for g in range(8):
            far = levels[np.abs(levels - a[p, g]) >= 10]
            a[p, g + 8] = far[np.random.randint(len(far))]
    return np.exp2(a.ravel()).repeat(32)


def f64(x):
    return np.asarray(x).astype(np.float64)


def striped(idx):
    return np.tile(np.asarray(idx).reshape(-1, 16).T, (8, 1)).astype(np.uint16)


def unstriped(offs):
    return offs[:16].T.reshape(-1).astype(np.int64)


def striped8(idx):
    return np.asarray(idx).reshape(8, -1, 16).transpose(0, 2, 1).reshape(128, -1).astype(np.uint16)


def unstriped8(offs):
    return offs.reshape(8, 16, -1).transpose(0, 2, 1).reshape(8, -1).astype(np.int64)


def pick8(x, idx, run):
    r = np.arange(len(x))
    return x[r[:, None], idx[r % (8 * run) // run]]


E2M1 = np.array([0.0, 0.5, 1.0, 1.5, 2.0, 3.0, 4.0, 6.0, -0.0, -0.5, -1.0, -1.5, -2.0, -3.0, -4.0, -6.0])


def pack_weight(w, fmt):
    k, n = w.shape
    w = f64(np.asarray(w, np.float32).astype(ml_dtypes.bfloat16)).reshape(k // 32, 32, n)
    amax = np.abs(w).max(1)
    if fmt == "e4m3":
        byte = np.frexp(amax)[1] - 1 + 127 - 7
    else:
        mant, ex = np.frexp(amax / 6.0)
        byte = np.where(mant > 0.5, ex, ex - 1) + 127
    byte = np.clip(np.where(amax > 0, byte, 1), 1, 254)
    scaled = (w * np.exp2(127.0 - byte)[:, None, :]).reshape(k, n).astype(np.float32)
    by_word = np.ascontiguousarray(scaled.reshape(k // 512, 128, 4, n).transpose(0, 1, 3, 2))
    if fmt == "e4m3":
        words = by_word.astype(ml_dtypes.float8_e4m3fn).view(np.uint8)
    else:
        c = by_word.astype(ml_dtypes.float4_e2m1fn).view(np.uint8) & 0xF
        words = (c[..., 0::2] | (c[..., 1::2] << 4)).reshape(k // 512, 128, 2 * n)
    return np.ascontiguousarray(words), np.ascontiguousarray(byte.astype(np.uint8).reshape(k // 512, 16, n))


def unpack_weight(words, scales, fmt):
    g, _, n = scales.shape
    words = np.ascontiguousarray(words).reshape(g, 128, n, -1)
    if fmt == "e4m3":
        vals = words.view(ml_dtypes.float8_e4m3fn).astype(np.float64)
    else:
        nib = np.empty((g, 128, n, 4), np.uint8)
        nib[..., 0::2] = words & 0xF
        nib[..., 1::2] = words >> 4
        vals = E2M1[nib]
    vals = vals * np.repeat(np.exp2(scales.astype(np.float64) - 127.0), 8, axis=1)[..., None]
    return vals.transpose(0, 1, 3, 2).reshape(g * 512, n)


def sigmoid(v):
    return 1.0 / (1.0 + np.exp(-v))


K, R, F, T, J, M = 512, 128, 512, 2048, 512, 256


def setup_inputs():
    n = np.random.standard_normal
    idx = np.random.permutation(T)[:J]
    idx2 = np.stack([np.random.permutation(J)[:M] for _ in range(8)])
    fk = mx_kscale(K)
    ff = mx_kscale(F)
    fj = mx_kscale(J)
    tj = np.ones(T)
    tj[idx] = fj
    tabp = pack_weight(n((K, T)) / fk[:, None], "e2m1")
    return {
        "tab_words": tabp[0],
        "tab_scales": tabp[1],
        "w1": (n((K, R)) * 1 / np.sqrt(K) * fk[:, None]).astype(np.float32),
        "bias": (np.random.uniform(-0.5, 0.5, (R, 1))).astype(np.float32),
        "gain": (np.random.uniform(0.5, 1.5, (R, 1))).astype(np.float32),
        "pw": (np.random.uniform(0.5, 1.5, (1, M))).astype(np.float32),
        "wo": (n((F, R)) * 1 / np.sqrt(F) * ff[:, None]).astype(np.float32),
        "dy": (n((F, M)) / ff[:, None]).astype(np.float32),
        "js": (np.random.uniform(0.5, 2.0, (1, J)) * fj).astype(np.float32),
        "xrows": (n((K, T)) / tj).astype(np.float32),
        "old": (n((K, R)) * 4.0).astype(np.float32),
        "offs": striped(idx),
        "offs2": striped8(idx2),
    }


def reference(tab_words, tab_scales, w1, bias, gain, pw, wo, dy, js, xrows, old, offs, offs2):
    idx = unstriped(offs)
    idx2 = unstriped8(offs2)
    tabu = unpack_weight(tab_words, tab_scales, "e2m1")
    w1q = mxq(f64(w1), 0, "e4m3")
    tabidxg = tabu[:, idx]
    a = w1q.T @ tabidxg
    h1 = np.tanh(a + f64(bias))
    h2 = h1 * f64(gain)
    s = pick8(h2, idx2, 16) * f64(pw)
    woq = mxq(f64(wo), 0, "e4m3")
    dyq = mxq(f64(dy), 0, "e4m3")
    c0 = woq.T @ dyq
    ds = c0 * sigmoid(s) * (1.0 + s * (1.0 - sigmoid(s)))
    e1 = ds * f64(pw)
    s1 = np.zeros((R, J))
    s1[np.arange(R)[:, None], idx2[np.arange(R) % 128 // 16]] = e1
    dh1 = s1 * f64(gain)
    da = dh1 * (1.0 - np.square(h1))
    gs = da * f64(js)
    gt1 = gs.T
    xt = f64(xrows)[:, idx].T
    xtq = mxq(xt, 0, "e4m3")
    gt1q = mxq(gt1, 0, "e4m3")
    gw = xtq.T @ gt1q
    y = gw + f64(old)
    return y

@@ -1,0 +1,183 @@
+from contextlib import ExitStack
+
+import concourse.mybir as mybir
+
+K, R, F, T, J, M = 512, 128, 512, 2048, 512, 256
+FLOPS = 2 * (K * R * J + F * R * M + J * K * R)
+
+F32 = mybir.dt.float32
+BF16 = mybir.dt.bfloat16
+I32 = mybir.dt.int32
+U32 = mybir.dt.uint32
+U16 = mybir.dt.uint16
+U8 = mybir.dt.uint8
+FP8X4 = mybir.dt.float8_e4m3fn_x4
+FP4X4 = mybir.dt.float4_e2m1fn_x4
+ACT = mybir.ActivationFunctionType
+ALU = mybir.AluOpType
+
+P = 128
+PACK = 4
+
+
+def interleaved_views(grouped, raw):
+    return (
+        grouped[:].rearrange("p (c i t) -> p c t i", i=4, t=PACK),
+        raw[:].rearrange("p t (c i) -> p c t i", i=4),
+    )
+
+
+def quantize(nc, pool, grouped, name, codes=None):
+    width = grouped.shape[1] // PACK
+    if codes is None:
+        codes = pool.tile([P, width], U32, name=name + "_codes", align_bytes=64)
+    scales = pool.tile([P, width], U8, name=name + "_scales", align_bytes=64)
+    nc.vector.quantize_mx(out=codes[:].bitcast(FP8X4), scales=scales[:], in_=grouped[:])
+    return codes, scales
+
+
+def turn(nc, grouped, bank, rows, identity):
+    words = rows[:].bitcast(F32)
+    for u in range(2):
+        nc.tensor.transpose(bank[:, u, :], words[:, u : J // 2 : 2], identity[:])
+    nc.scalar.copy(
+        grouped.bitcast(F32).rearrange("p (c u) -> p c u", u=2),
+        bank[:].rearrange("p u c -> p c u"),
+    )
+
+
+def tile_attend_cpickact_w_kernel(tc, tab_words, tab_scales, w1, bias, gain, pw, wo, dy, js, xrows, old, offs, offs2, out):
+    nc = tc.nc
+    with ExitStack() as ctx:
+        keep = ctx.enter_context(tc.tile_pool(name="keep", bufs=1))
+        sb = ctx.enter_context(tc.tile_pool(name="sb", bufs=1))
+        ps = ctx.enter_context(tc.psum_pool(name="ps", bufs=1))
+
+        slots = keep.tile([P, J // 16], U16, name="slots")
+        nc.sync.dma_start(slots[:], offs)
+        picks = keep.tile([P, M // 16], U16, name="picks")
+        nc.sync.dma_start(picks[:], offs2)
+        w1_raw = keep.tile([P, PACK, R], F32, name="w1_raw")
+        nc.sync.dma_start(w1_raw[:], w1.rearrange("(p t) r -> p t r", t=PACK))
+        tab_s = keep.tile([P, T], U8, name="tab_s")
+        nc.vector.memset(tab_s[:, 0 : T // 2].bitcast(I32), 0)
+        nc.gpsimd.memset(tab_s[:, T // 2 : T].bitcast(I32), 0)
+        for q in range(4):
+            nc.sync.dma_start(tab_s[32 * q : 32 * q + 4, :].bitcast(I32), tab_scales[0, 4 * q : 4 * q + 4, :].bitcast(I32))
+
+        identity = keep.tile([P, P], F32, name="identity")
+        with tc.tile_pool(name="early", bufs=1) as early:
+            zeros = early.tile([P, 13 * 1024], F32, name="zeros")
+            nc.gpsimd.memset(zeros[:, 0:P], 0.0)
+            nc.gpsimd.affine_select(out=identity[:], in_=zeros[:, 0:P], compare_op=ALU.not_equal, fill=1.0, base=0,
+                                    pattern=[[-1, P]], channel_multiplier=1)
+
+        late = ctx.enter_context(tc.tile_pool(name="late", bufs=1))
+        tab_w = late.tile([P, T], U16, name="tab_w")
+        nc.sync.dma_start(tab_w[:].bitcast(I32), tab_words[0].bitcast(I32))
+        wo_raw = late.tile([P, PACK, R], F32, name="wo_raw")
+        nc.sync.dma_start(wo_raw[:], wo.rearrange("(p t) r -> p t r", t=PACK))
+        bias_col = late.tile([P, 1], F32, name="bias_col")
+        nc.sync.dma_start(bias_col[:], bias)
+        pw_cols = late.tile([P, 2], F32, name="pw_cols")
+        nc.sync.dma_start(pw_cols[:], pw.rearrange("o (p e) -> (o p) e", e=2))
+        gain_col = late.tile([P, 1], F32, name="gain_col")
+        nc.sync.dma_start(gain_col[:], gain)
+        js_cols = late.tile([P, 4], F32, name="js_cols")
+        nc.sync.dma_start(js_cols[:], js.rearrange("o (p e) -> (o p) e", e=4))
+        dy_raw = late.tile([P, PACK, M], F32, name="dy_raw")
+        nc.sync.dma_start(dy_raw[:], dy.rearrange("(p t) m -> p t m", t=PACK))
+        x_rows = xrows.rearrange("(p b) t -> p b t", b=4)
+        x_tiles = [late.tile([P, T], F32, name=f"x{b}", tag=f"x{b}", align_bytes=64) for b in range(4)]
+        for b in range(4):
+            nc.sync.dma_start(x_tiles[b][:], x_rows[:, b, :])
+        old_sb = late.tile([P, 4, R], F32, name="old_sb")
+        nc.sync.dma_start(old_sb[:], old.rearrange("(p b) r -> p b r", b=4))
+
+        s1 = sb.tile([P, J], F32, name="s1", tag="reuse3")
+        nc.vector.memset(s1[:], 0.0)
+
+        tab_sg = sb.tile([P, J], U8, name="tab_sg", align_bytes=64)
+        nc.vector.tensor_copy(tab_sg[:], tab_s[:].indirect(slots[:]))
+        tab_wg = sb.tile([P, J], U16, name="tab_wg", align_bytes=64)
+        nc.vector.tensor_copy(tab_wg[:], tab_w[:].indirect(slots[:]))
+        w1_grouped = sb.tile([P, R * PACK], BF16, name="w1_grouped", align_bytes=64)
+        nc.scalar.activation(*interleaved_views(w1_grouped, w1_raw), ACT.Copy)
+        w1_codes, w1_scales = quantize(nc, sb, w1_grouped, "w1")
+        a_ps = ps.tile([P, J], F32, name="a_ps", tag="bank0")
+        pw_ps = a_ps[:, 0:M].rearrange("p (e c) -> p e c", e=2)
+        for e in range(2):
+            nc.tensor.transpose(pw_ps[:, e, :], pw_cols[:, e : e + 1].to_broadcast([P, P]), identity[:])
+        half_pw = sb.tile([P, M], F32, name="half_pw")
+        nc.scalar.activation(half_pw[:].rearrange("p (c e) -> p c e", e=2), pw_ps.rearrange("p e c -> p c e"), ACT.Copy, scale=0.5)
+
+        nc.tensor.matmul_mx(out=a_ps[:], lhsT=w1_codes[:].bitcast(FP8X4), lhsT_scale=w1_scales[:],
+                            rhs=tab_wg[:].bitcast(FP4X4), rhs_scale=tab_sg[:], start=True, stop=True)
+
+        wo_grouped = sb.tile([P, R * PACK], BF16, name="wo_grouped", align_bytes=64)
+        nc.scalar.activation(*interleaved_views(wo_grouped, wo_raw), ACT.Copy)
+        dy_grouped = sb.tile([P, M * PACK], BF16, name="dy_grouped", align_bytes=64)
+        nc.vector.tensor_copy(*interleaved_views(dy_grouped, dy_raw))
+        wo_codes, wo_scales = quantize(nc, sb, wo_grouped, "wo")
+        dy_codes, dy_scales = quantize(nc, sb, dy_grouped, "dy")
+        js_ps = ps.tile([P, 4, P], F32, name="js_ps", tag="bank3")
+        for e in range(4):
+            nc.tensor.transpose(js_ps[:, e, :], js_cols[:, e : e + 1].to_broadcast([P, P]), identity[:])
+        gain_js = sb.tile([P, J], F32, name="gain_js")
+        nc.scalar.activation(gain_js[:].rearrange("p (c e) -> p c e", e=4), js_ps[:].rearrange("p e c -> p c e"), ACT.Copy, scale=gain_col[:])
+        c0_ps = js_ps[:, 0:2, :].rearrange("p e c -> p (e c)")
+        nc.tensor.matmul_mx(out=c0_ps, lhsT=wo_codes[:].bitcast(FP8X4), lhsT_scale=wo_scales[:],
+                            rhs=dy_codes[:].bitcast(FP8X4), rhs_scale=dy_scales[:], start=True, stop=True)
+
+        h1 = sb.tile([P, J], F32, name="h1")
+        nc.scalar.activation(h1[:], a_ps[:], ACT.Tanh, bias=bias_col[:])
+        h2 = sb.tile([P, J], F32, name="h2")
+        nc.scalar.activation(h2[:], h1[:], ACT.Copy, scale=gain_col[:])
+        half_s = sb.tile([P, M], F32, name="half_s")
+        nc.vector.tensor_tensor(half_s[:], h2[:].indirect(picks[:]), half_pw[:], ALU.mult)
+        c0_pw = sb.tile([P, M], F32, name="c0_pw")
+        nc.vector.tensor_tensor(c0_pw[:], c0_ps, half_pw[:], ALU.mult)
+        xg0 = half_pw[:].bitcast(BF16)
+        nc.vector.tensor_copy(xg0[:], x_tiles[0][:].indirect(slots[:]))
+        h1_sq = sb.tile([P, J], F32, name="h1_sq")
+        nc.scalar.activation(h1_sq[:], h1[:], ACT.Square)
+        th = sb.tile([P, M], F32, name="th")
+        nc.scalar.activation(th[:], half_s[:], ACT.Tanh)
+        th_sq = sb.tile([P, M], F32, name="th_sq")
+        nc.scalar.activation(th_sq[:], th[:], ACT.Square)
+
+        bend = late.tile([P, M], F32, name="bend", tag="x0", align_bytes=64)
+        nc.vector.scalar_tensor_tensor(bend[:], th_sq[:], 1.0, half_s[:], ALU.subtract, ALU.mult)
+        slope2 = sb.tile([P, M], F32, name="slope2")
+        nc.vector.scalar_tensor_tensor(slope2[:], th[:], 1.0, bend[:], ALU.add, ALU.subtract)
+        nc.vector.tensor_tensor(s1[:].indirect(picks[:]), slope2[:], c0_pw[:], ALU.mult)
+
+        neg_factor = sb.tile([P, J], F32, name="neg_factor")
+        nc.vector.scalar_tensor_tensor(neg_factor[:], h1_sq[:], 1.0, gain_js[:], ALU.subtract, ALU.mult)
+        gs = sb.tile([P, J], BF16, name="gs")
+        nc.vector.scalar_tensor_tensor(gs[:], s1[:], -1.0, neg_factor[:], ALU.mult, ALU.mult)
+
+        out_rows = out.rearrange("(p b) r -> p b r", b=4)
+        xg = [xg0, c0_pw[:].bitcast(BF16), neg_factor[:, 0:M].bitcast(BF16), sb.tile([P, J], BF16, name="xg3", tag="reuse3")]
+        for b in (1, 2, 3):
+            nc.vector.tensor_copy(xg[b][:], x_tiles[b][:].indirect(slots[:]))
+        early = sb.tile([P, 2 * J], BF16, name="early", align_bytes=64)
+        xt_mid = sb.tile([P, 2 * J], BF16, name="xt_mid", align_bytes=64)
+        xt_last = sb.tile([P, J], BF16, name="xt_last", align_bytes=64)
+        places = (early[:, 0:J], early[:, J : 2 * J], xt_mid[:, 0:J], xt_mid[:, J : 2 * J], xt_last[:])
+        for n, rows in enumerate((xg[0], gs, xg[1], xg[2], xg[3])):
+            turned = ps.tile([P, 2, P], F32, name=f"turned{n}", tag=("bank5", "bank4", "bank6", "bank1", "bank2")[n])
+            turn(nc, places[n], turned, rows, identity)
+        early_codes, early_scales = quantize(nc, sb, early, "early", late.tile([P, 2 * P], U32, name="early_codes", tag="x2", align_bytes=64))
+        mid_codes, mid_scales = quantize(nc, sb, xt_mid, "xt_mid", late.tile([P, 2 * P], U32, name="mid_codes", tag="x3", align_bytes=64))
+        last_codes, last_scales = quantize(nc, sb, xt_last, "xt_last")
+        codes = (early_codes[:, 0:P], mid_codes[:, 0:P], mid_codes[:, P : 2 * P], last_codes[:])
+        scales = (early_scales[:, 0:P], mid_scales[:, 0:P], mid_scales[:, P : 2 * P], last_scales[:])
+        for b0, b1, tag in ((0, 3, "bank7"), (3, 4, "bank0")):
+            gw_ps = ps.tile([P, b1 - b0, R], F32, name=f"gw_ps{b0}", tag=tag)
+            for b in range(b0, b1):
+                nc.tensor.matmul_mx(out=gw_ps[:, b - b0, :], lhsT=codes[b].bitcast(FP8X4), lhsT_scale=scales[b],
+                                    rhs=early_codes[:, P : 2 * P].bitcast(FP8X4), rhs_scale=early_scales[:, P : 2 * P], start=True, stop=True)
+            y = sb.tile([P, b1 - b0, R], F32, name=f"y{b0}")
+            nc.vector.tensor_tensor(y[:], gw_ps[:], old_sb[:, b0:b1, :], ALU.add)
+            nc.sync.dma_start(out_rows[:, b0:b1, :], y[:])

@@ -1,6 +1,7 @@
 from contextlib import ExitStack
 
 import concourse.mybir as mybir
+from concourse.masks import make_identity
 
 K, R, F, T, J, M = 512, 128, 512, 2048, 512, 256
 FLOPS = 2 * (K * R * J + F * R * M + J * K * R)
@@ -18,6 +19,7 @@ ALU = mybir.AluOpType
 
 P = 128
 PACK = 4
+HALF = J // 2
 
 
 def interleaved_views(grouped, raw):
@@ -37,7 +39,7 @@ def quantize(nc, pool, grouped, name, codes=None):
 
 
 def turn(nc, grouped, bank, rows, identity):
-    words = rows[:].bitcast(F32)
+    words = rows.bitcast(F32)
     for u in range(2):
         nc.tensor.transpose(bank[:, u, :], words[:, u : J // 2 : 2], identity[:])
     nc.scalar.copy(
@@ -49,135 +51,136 @@ def turn(nc, grouped, bank, rows, identity):
 def tile_attend_cpickact_w_kernel(tc, tab_words, tab_scales, w1, bias, gain, pw, wo, dy, js, xrows, old, offs, offs2, out):
     nc = tc.nc
     with ExitStack() as ctx:
-        keep = ctx.enter_context(tc.tile_pool(name="keep", bufs=1))
         sb = ctx.enter_context(tc.tile_pool(name="sb", bufs=1))
         ps = ctx.enter_context(tc.psum_pool(name="ps", bufs=1))
 
-        slots = keep.tile([P, J // 16], U16, name="slots")
+        slots = sb.tile([P, J // 16], U16, name="slots")
         nc.sync.dma_start(slots[:], offs)
-        picks = keep.tile([P, M // 16], U16, name="picks")
+        picks = sb.tile([P, M // 16], U16, name="picks")
         nc.sync.dma_start(picks[:], offs2)
-        w1_raw = keep.tile([P, PACK, R], F32, name="w1_raw")
-        nc.sync.dma_start(w1_raw[:], w1.rearrange("(p t) r -> p t r", t=PACK))
-        tab_s = keep.tile([P, T], U8, name="tab_s")
+        tab_w = sb.tile([P, T], U16, name="tab_w", tag="tab_w", align_bytes=64)
+        nc.sync.dma_start(tab_w[:].bitcast(I32), tab_words[0].bitcast(I32))
+        tab_s = sb.tile([P, T], U8, name="tab_s")
         nc.vector.memset(tab_s[:, 0 : T // 2].bitcast(I32), 0)
         nc.gpsimd.memset(tab_s[:, T // 2 : T].bitcast(I32), 0)
         for q in range(4):
             nc.sync.dma_start(tab_s[32 * q : 32 * q + 4, :].bitcast(I32), tab_scales[0, 4 * q : 4 * q + 4, :].bitcast(I32))
 
-        identity = keep.tile([P, P], F32, name="identity")
-        with tc.tile_pool(name="early", bufs=1) as early:
-            zeros = early.tile([P, 13 * 1024], F32, name="zeros")
-            nc.gpsimd.memset(zeros[:, 0:P], 0.0)
-            nc.gpsimd.affine_select(out=identity[:], in_=zeros[:, 0:P], compare_op=ALU.not_equal, fill=1.0, base=0,
-                                    pattern=[[-1, P]], channel_multiplier=1)
+        identity = sb.tile([P, P], F32, name="identity")
+        make_identity(nc, identity[:])
 
-        late = ctx.enter_context(tc.tile_pool(name="late", bufs=1))
-        tab_w = late.tile([P, T], U16, name="tab_w")
-        nc.sync.dma_start(tab_w[:].bitcast(I32), tab_words[0].bitcast(I32))
-        wo_raw = late.tile([P, PACK, R], F32, name="wo_raw")
-        nc.sync.dma_start(wo_raw[:], wo.rearrange("(p t) r -> p t r", t=PACK))
-        bias_col = late.tile([P, 1], F32, name="bias_col")
-        nc.sync.dma_start(bias_col[:], bias)
-        pw_cols = late.tile([P, 2], F32, name="pw_cols")
+        w1_raw = sb.tile([P, PACK, R], F32, name="w1_raw", tag="w1_raw", align_bytes=64)
+        nc.sync.dma_start(w1_raw[:], w1.rearrange("(p t) r -> p t r", t=PACK))
+        pw_cols = sb.tile([P, 2], F32, name="pw_cols")
         nc.sync.dma_start(pw_cols[:], pw.rearrange("o (p e) -> (o p) e", e=2))
-        gain_col = late.tile([P, 1], F32, name="gain_col")
+        wo_raw = sb.tile([P, PACK, R], F32, name="wo_raw", tag="wo_raw", align_bytes=64)
+        nc.sync.dma_start(wo_raw[:], wo.rearrange("(p t) r -> p t r", t=PACK))
+        bias_col = sb.tile([P, 1], F32, name="bias_col")
+        nc.sync.dma_start(bias_col[:], bias)
+        gain_col = sb.tile([P, 1], F32, name="gain_col")
         nc.sync.dma_start(gain_col[:], gain)
-        js_cols = late.tile([P, 4], F32, name="js_cols")
+        js_cols = sb.tile([P, 4], F32, name="js_cols")
         nc.sync.dma_start(js_cols[:], js.rearrange("o (p e) -> (o p) e", e=4))
-        dy_raw = late.tile([P, PACK, M], F32, name="dy_raw")
+        dy_raw = sb.tile([P, PACK, M], F32, name="dy_raw")
         nc.sync.dma_start(dy_raw[:], dy.rearrange("(p t) m -> p t m", t=PACK))
         x_rows = xrows.rearrange("(p b) t -> p b t", b=4)
-        x_tiles = [late.tile([P, T], F32, name=f"x{b}", tag=f"x{b}", align_bytes=64) for b in range(4)]
+        x_tiles = [sb.tile([P, T], F32, name=f"x{b}", tag=f"x{b}", align_bytes=64) for b in range(4)]
         for b in range(4):
             nc.sync.dma_start(x_tiles[b][:], x_rows[:, b, :])
-        old_sb = late.tile([P, 4, R], F32, name="old_sb")
+        old_sb = sb.tile([P, 4, R], F32, name="old_sb")
         nc.sync.dma_start(old_sb[:], old.rearrange("(p b) r -> p b r", b=4))
 
-        s1 = sb.tile([P, J], F32, name="s1", tag="reuse3")
+        s1 = sb.tile([P, J], F32, name="s1", tag="s1")
         nc.vector.memset(s1[:], 0.0)
 
-        tab_sg = sb.tile([P, J], U8, name="tab_sg", align_bytes=64)
-        nc.vector.tensor_copy(tab_sg[:], tab_s[:].indirect(slots[:]))
-        tab_wg = sb.tile([P, J], U16, name="tab_wg", align_bytes=64)
-        nc.vector.tensor_copy(tab_wg[:], tab_w[:].indirect(slots[:]))
         w1_grouped = sb.tile([P, R * PACK], BF16, name="w1_grouped", align_bytes=64)
         nc.scalar.activation(*interleaved_views(w1_grouped, w1_raw), ACT.Copy)
         w1_codes, w1_scales = quantize(nc, sb, w1_grouped, "w1")
-        a_ps = ps.tile([P, J], F32, name="a_ps", tag="bank0")
-        pw_ps = a_ps[:, 0:M].rearrange("p (e c) -> p e c", e=2)
+        js_ps = ps.tile([P, 4, P], F32, name="js_ps", tag="bank0")
+        pw_ps = ps.tile([P, 2, P], F32, name="pw_ps", tag="bank1")
+        a_ps = [bank[:, 0:2, :].rearrange("p e c -> p (e c)") for bank in (pw_ps, js_ps)]
         for e in range(2):
             nc.tensor.transpose(pw_ps[:, e, :], pw_cols[:, e : e + 1].to_broadcast([P, P]), identity[:])
         half_pw = sb.tile([P, M], F32, name="half_pw")
-        nc.scalar.activation(half_pw[:].rearrange("p (c e) -> p c e", e=2), pw_ps.rearrange("p e c -> p c e"), ACT.Copy, scale=0.5)
+        nc.scalar.activation(half_pw[:].rearrange("p (c e) -> p c e", e=2), pw_ps[:].rearrange("p e c -> p c e"), ACT.Copy, scale=0.5)
 
-        nc.tensor.matmul_mx(out=a_ps[:], lhsT=w1_codes[:].bitcast(FP8X4), lhsT_scale=w1_scales[:],
-                            rhs=tab_wg[:].bitcast(FP4X4), rhs_scale=tab_sg[:], start=True, stop=True)
+        tab_wg = [sb.tile([P, HALF], U16, name="tab_wg0", align_bytes=64), sb.tile([P, HALF], U16, name="tab_wg1", tag="w1_raw", align_bytes=64)]
+        tab_sg = sb.tile([P, J], U8, name="tab_sg", align_bytes=64)
+        h1 = sb.tile([P, J], F32, name="h1")
+        h2 = sb.tile([P, J], F32, name="h2")
+        for h in range(2):
+            cols = slice(h * HALF, (h + 1) * HALF)
+            part = slots[:, h * HALF // 16 : (h + 1) * HALF // 16]
+            nc.vector.tensor_copy(tab_wg[h][:], tab_w[:].indirect(part))
+            nc.vector.tensor_copy(tab_sg[:, cols], tab_s[:].indirect(part))
+            nc.tensor.matmul_mx(out=a_ps[h], lhsT=w1_codes[:].bitcast(FP8X4), lhsT_scale=w1_scales[:],
+                                rhs=tab_wg[h][:].bitcast(FP4X4), rhs_scale=tab_sg[:, cols], start=True, stop=True)
+            nc.scalar.activation(h1[:, cols], a_ps[h], ACT.Tanh, bias=bias_col[:])
+            nc.scalar.activation(h2[:, cols], h1[:, cols], ACT.Copy, scale=gain_col[:])
 
         wo_grouped = sb.tile([P, R * PACK], BF16, name="wo_grouped", align_bytes=64)
         nc.scalar.activation(*interleaved_views(wo_grouped, wo_raw), ACT.Copy)
-        dy_grouped = sb.tile([P, M * PACK], BF16, name="dy_grouped", align_bytes=64)
+        dy_grouped = sb.tile([P, M * PACK], BF16, name="dy_grouped", tag="tab_w", align_bytes=64)
         nc.vector.tensor_copy(*interleaved_views(dy_grouped, dy_raw))
         wo_codes, wo_scales = quantize(nc, sb, wo_grouped, "wo")
         dy_codes, dy_scales = quantize(nc, sb, dy_grouped, "dy")
-        js_ps = ps.tile([P, 4, P], F32, name="js_ps", tag="bank3")
+        c0_ps = ps.tile([P, M], F32, name="c0_ps", tag="bank2")
+        nc.tensor.matmul_mx(out=c0_ps[:], lhsT=wo_codes[:].bitcast(FP8X4), lhsT_scale=wo_scales[:],
+                            rhs=dy_codes[:].bitcast(FP8X4), rhs_scale=dy_scales[:], start=True, stop=True)
+
+        half_s = wo_raw[:, 0:2, :].rearrange("p t r -> p (t r)")
+        nc.vector.tensor_tensor(half_s[:], h2[:].indirect(picks[:]), half_pw[:], ALU.mult)
+        c0_pw = sb.tile([P, M], F32, name="c0_pw")
+        nc.vector.tensor_tensor(c0_pw[:], c0_ps[:], half_pw[:], ALU.mult)
+        xg0 = half_pw[:].bitcast(BF16)
+        nc.vector.tensor_copy(xg0, x_tiles[0][:].indirect(slots[:]))
+        th = sb.tile([P, M], F32, name="th")
+        th_sq = sb.tile([P, M], F32, name="th_sq")
+        nc.scalar.activation(th[:], half_s[:], ACT.Tanh)
+        nc.scalar.activation(th_sq[:], th[:], ACT.Square)
+        h1_sq = sb.tile([P, J], F32, name="h1_sq")
+        nc.scalar.activation(h1_sq[:], h1[:], ACT.Square)
         for e in range(4):
             nc.tensor.transpose(js_ps[:, e, :], js_cols[:, e : e + 1].to_broadcast([P, P]), identity[:])
         gain_js = sb.tile([P, J], F32, name="gain_js")
         nc.scalar.activation(gain_js[:].rearrange("p (c e) -> p c e", e=4), js_ps[:].rearrange("p e c -> p c e"), ACT.Copy, scale=gain_col[:])
-        c0_ps = js_ps[:, 0:2, :].rearrange("p e c -> p (e c)")
-        nc.tensor.matmul_mx(out=c0_ps, lhsT=wo_codes[:].bitcast(FP8X4), lhsT_scale=wo_scales[:],
-                            rhs=dy_codes[:].bitcast(FP8X4), rhs_scale=dy_scales[:], start=True, stop=True)
 
-        h1 = sb.tile([P, J], F32, name="h1")
-        nc.scalar.activation(h1[:], a_ps[:], ACT.Tanh, bias=bias_col[:])
-        h2 = sb.tile([P, J], F32, name="h2")
-        nc.scalar.activation(h2[:], h1[:], ACT.Copy, scale=gain_col[:])
-        half_s = sb.tile([P, M], F32, name="half_s")
-        nc.vector.tensor_tensor(half_s[:], h2[:].indirect(picks[:]), half_pw[:], ALU.mult)
-        c0_pw = sb.tile([P, M], F32, name="c0_pw")
-        nc.vector.tensor_tensor(c0_pw[:], c0_ps, half_pw[:], ALU.mult)
-        xg0 = half_pw[:].bitcast(BF16)
-        nc.vector.tensor_copy(xg0[:], x_tiles[0][:].indirect(slots[:]))
-        h1_sq = sb.tile([P, J], F32, name="h1_sq")
-        nc.scalar.activation(h1_sq[:], h1[:], ACT.Square)
-        th = sb.tile([P, M], F32, name="th")
-        nc.scalar.activation(th[:], half_s[:], ACT.Tanh)
-        th_sq = sb.tile([P, M], F32, name="th_sq")
-        nc.scalar.activation(th_sq[:], th[:], ACT.Square)
-
-        bend = late.tile([P, M], F32, name="bend", tag="x0", align_bytes=64)
+        after_x0 = sb.tile([P, M + J], F32, name="after_x0", tag="x0", align_bytes=64)
+        bend, neg_all = after_x0[:, 0:M], after_x0[:, M : M + J]
         nc.vector.scalar_tensor_tensor(bend[:], th_sq[:], 1.0, half_s[:], ALU.subtract, ALU.mult)
         slope2 = sb.tile([P, M], F32, name="slope2")
         nc.vector.scalar_tensor_tensor(slope2[:], th[:], 1.0, bend[:], ALU.add, ALU.subtract)
+        nc.vector.scalar_tensor_tensor(neg_all[:], h1_sq[:], 1.0, gain_js[:], ALU.subtract, ALU.mult)
         nc.vector.tensor_tensor(s1[:].indirect(picks[:]), slope2[:], c0_pw[:], ALU.mult)
-
-        neg_factor = sb.tile([P, J], F32, name="neg_factor")
-        nc.vector.scalar_tensor_tensor(neg_factor[:], h1_sq[:], 1.0, gain_js[:], ALU.subtract, ALU.mult)
-        gs = sb.tile([P, J], BF16, name="gs")
-        nc.vector.scalar_tensor_tensor(gs[:], s1[:], -1.0, neg_factor[:], ALU.mult, ALU.mult)
+        xg2 = c0_pw[:].bitcast(BF16)
+        nc.vector.tensor_copy(xg2, x_tiles[2][:].indirect(slots[:]))
+        gs = sb.tile([P, J], BF16, name="gs", tag="x2", align_bytes=64)
+        nc.vector.scalar_tensor_tensor(gs[:], s1[:], -1.0, neg_all[:], ALU.mult, ALU.mult)
 
         out_rows = out.rearrange("(p b) r -> p b r", b=4)
-        xg = [xg0, c0_pw[:].bitcast(BF16), neg_factor[:, 0:M].bitcast(BF16), sb.tile([P, J], BF16, name="xg3", tag="reuse3")]
-        for b in (1, 2, 3):
-            nc.vector.tensor_copy(xg[b][:], x_tiles[b][:].indirect(slots[:]))
-        early = sb.tile([P, 2 * J], BF16, name="early", align_bytes=64)
-        xt_mid = sb.tile([P, 2 * J], BF16, name="xt_mid", align_bytes=64)
-        xt_last = sb.tile([P, J], BF16, name="xt_last", align_bytes=64)
-        places = (early[:, 0:J], early[:, J : 2 * J], xt_mid[:, 0:J], xt_mid[:, J : 2 * J], xt_last[:])
-        for n, rows in enumerate((xg[0], gs, xg[1], xg[2], xg[3])):
-            turned = ps.tile([P, 2, P], F32, name=f"turned{n}", tag=("bank5", "bank4", "bank6", "bank1", "bank2")[n])
-            turn(nc, places[n], turned, rows, identity)
-        early_codes, early_scales = quantize(nc, sb, early, "early", late.tile([P, 2 * P], U32, name="early_codes", tag="x2", align_bytes=64))
-        mid_codes, mid_scales = quantize(nc, sb, xt_mid, "xt_mid", late.tile([P, 2 * P], U32, name="mid_codes", tag="x3", align_bytes=64))
-        last_codes, last_scales = quantize(nc, sb, xt_last, "xt_last")
-        codes = (early_codes[:, 0:P], mid_codes[:, 0:P], mid_codes[:, P : 2 * P], last_codes[:])
-        scales = (early_scales[:, 0:P], mid_scales[:, 0:P], mid_scales[:, P : 2 * P], last_scales[:])
-        for b0, b1, tag in ((0, 3, "bank7"), (3, 4, "bank0")):
+        xg = [xg0, sb.tile([P, J], BF16, name="xg1")[:], xg2, sb.tile([P, J], BF16, name="xg3", tag="s1")[:]]
+        x1_bf = sb.tile([P, T], BF16, name="x1_bf", tag="wo_raw", align_bytes=64)
+        nc.scalar.activation(x1_bf[:], x_tiles[1][:], ACT.Copy)
+        nc.scalar.activation(xg[1], x1_bf[:].indirect(slots[:]), ACT.Copy)
+        nc.vector.tensor_copy(xg[3], x_tiles[3][:].indirect(slots[:]))
+        early_in = sb.tile([P, 4 * J], BF16, name="early_in", align_bytes=64)
+        last_in = sb.tile([P, J], BF16, name="last_in", tag="y0", align_bytes=64)
+        banks = [ps.tile([P, 2, P], F32, name=f"turned{n}", tag=f"bank{4 + n}") for n in range(4)]
+        turn(nc, early_in[:, 0:J], banks[0], xg[0], identity)
+        turn(nc, early_in[:, J : 2 * J], banks[1], xg[1], identity)
+        turn(nc, early_in[:, 2 * J : 3 * J], banks[1], xg[2], identity)
+        turn(nc, early_in[:, 3 * J : 4 * J], banks[2], gs[:], identity)
+        turn(nc, last_in[:], banks[3], xg[3], identity)
+        early_codes, early_scales = quantize(nc, sb, early_in, "early", sb.tile([P, 4 * P], U32, name="early_codes", tag="x3", align_bytes=64))
+        last_codes, last_scales = quantize(nc, sb, last_in, "last")
+        codes = [early_codes[:, b * P : (b + 1) * P] for b in range(3)] + [last_codes[:]]
+        scales = [early_scales[:, b * P : (b + 1) * P] for b in range(3)] + [last_scales[:]]
+        gt_codes, gt_scales = early_codes[:, 3 * P : 4 * P], early_scales[:, 3 * P : 4 * P]
+        for b0, b1, tag in ((0, 3, "bank2"), (3, 4, "bank3")):
             gw_ps = ps.tile([P, b1 - b0, R], F32, name=f"gw_ps{b0}", tag=tag)
             for b in range(b0, b1):
                 nc.tensor.matmul_mx(out=gw_ps[:, b - b0, :], lhsT=codes[b].bitcast(FP8X4), lhsT_scale=scales[b],
-                                    rhs=early_codes[:, P : 2 * P].bitcast(FP8X4), rhs_scale=early_scales[:, P : 2 * P], start=True, stop=True)
-            y = sb.tile([P, b1 - b0, R], F32, name=f"y{b0}")
+                                    rhs=gt_codes.bitcast(FP8X4), rhs_scale=gt_scales, start=True, stop=True)
+            y = sb.tile([P, b1 - b0, R], F32, name=f"y{b0}", tag=f"y{b0}", align_bytes=64)
             nc.vector.tensor_tensor(y[:], gw_ps[:], old_sb[:, b0:b1, :], ALU.add)
             nc.sync.dma_start(out_rows[:, b0:b1, :], y[:])

@@ -38,13 +38,14 @@ def quantize(nc, pool, grouped, name, codes=None):
     return codes, scales
 
 
-def turn(nc, grouped, bank, rows, identity):
-    words = rows.bitcast(F32)
-    for u in range(2):
-        nc.tensor.transpose(bank[:, u, :], words[:, u : J // 2 : 2], identity[:])
+def turn(nc, grouped, bank, sources, identity):
+    for n, rows in enumerate(sources):
+        words = rows.bitcast(F32)
+        for u in range(2):
+            nc.tensor.transpose(bank[:, n, u, :], words[:, u : J // 2 : 2], identity[:])
     nc.scalar.copy(
-        grouped.bitcast(F32).rearrange("p (c u) -> p c u", u=2),
-        bank[:].rearrange("p u c -> p c u"),
+        grouped.bitcast(F32).rearrange("p (n c u) -> p n c u", n=len(sources), u=2),
+        bank[:].rearrange("p n u c -> p n c u"),
     )
 
 
@@ -73,7 +74,7 @@ def tile_attend_cpickact_w_kernel(tc, tab_words, tab_scales, w1, bias, gain, pw,
         nc.sync.dma_start(w1_raw[:], w1.rearrange("(p t) r -> p t r", t=PACK))
         pw_cols = sb.tile([P, 2], F32, name="pw_cols")
         nc.sync.dma_start(pw_cols[:], pw.rearrange("o (p e) -> (o p) e", e=2))
-        wo_raw = sb.tile([P, PACK, R], F32, name="wo_raw", tag="wo_raw", align_bytes=64)
+        wo_raw = sb.tile([P, PACK, R], F32, name="wo_raw")
         nc.sync.dma_start(wo_raw[:], wo.rearrange("(p t) r -> p t r", t=PACK))
         bias_col = sb.tile([P, 1], F32, name="bias_col")
         nc.sync.dma_start(bias_col[:], bias)
@@ -90,19 +91,19 @@ def tile_attend_cpickact_w_kernel(tc, tab_words, tab_scales, w1, bias, gain, pw,
         old_sb = sb.tile([P, 4, R], F32, name="old_sb")
         nc.sync.dma_start(old_sb[:], old.rearrange("(p b) r -> p b r", b=4))
 
-        s1 = sb.tile([P, J], F32, name="s1", tag="s1")
+        s1 = sb.tile([P, J], F32, name="s1")
         nc.vector.memset(s1[:], 0.0)
 
         w1_grouped = sb.tile([P, R * PACK], BF16, name="w1_grouped", align_bytes=64)
         nc.scalar.activation(*interleaved_views(w1_grouped, w1_raw), ACT.Copy)
         w1_codes, w1_scales = quantize(nc, sb, w1_grouped, "w1")
         js_ps = ps.tile([P, 4, P], F32, name="js_ps", tag="bank0")
-        pw_ps = ps.tile([P, 2, P], F32, name="pw_ps", tag="bank1")
+        pw_ps = ps.tile([P, 4, P], F32, name="pw_ps", tag="bank1")
         a_ps = [bank[:, 0:2, :].rearrange("p e c -> p (e c)") for bank in (pw_ps, js_ps)]
         for e in range(2):
             nc.tensor.transpose(pw_ps[:, e, :], pw_cols[:, e : e + 1].to_broadcast([P, P]), identity[:])
         half_pw = sb.tile([P, M], F32, name="half_pw")
-        nc.scalar.activation(half_pw[:].rearrange("p (c e) -> p c e", e=2), pw_ps[:].rearrange("p e c -> p c e"), ACT.Copy, scale=0.5)
+        nc.scalar.activation(half_pw[:].rearrange("p (c e) -> p c e", e=2), pw_ps[:, 0:2, :].rearrange("p e c -> p c e"), ACT.Copy, scale=0.5)
 
         tab_wg = [sb.tile([P, HALF], U16, name="tab_wg0", align_bytes=64), sb.tile([P, HALF], U16, name="tab_wg1", tag="w1_raw", align_bytes=64)]
         tab_sg = sb.tile([P, J], U8, name="tab_sg", align_bytes=64)
@@ -124,58 +125,62 @@ def tile_attend_cpickact_w_kernel(tc, tab_words, tab_scales, w1, bias, gain, pw,
         nc.vector.tensor_copy(*interleaved_views(dy_grouped, dy_raw))
         wo_codes, wo_scales = quantize(nc, sb, wo_grouped, "wo")
         dy_codes, dy_scales = quantize(nc, sb, dy_grouped, "dy")
-        c0_ps = ps.tile([P, M], F32, name="c0_ps", tag="bank2")
-        nc.tensor.matmul_mx(out=c0_ps[:], lhsT=wo_codes[:].bitcast(FP8X4), lhsT_scale=wo_scales[:],
+        c0_ps = a_ps[1]
+        nc.tensor.matmul_mx(out=c0_ps, lhsT=wo_codes[:].bitcast(FP8X4), lhsT_scale=wo_scales[:],
                             rhs=dy_codes[:].bitcast(FP8X4), rhs_scale=dy_scales[:], start=True, stop=True)
 
-        half_s = wo_raw[:, 0:2, :].rearrange("p t r -> p (t r)")
+        half_s = dy_grouped[:, 0 : 2 * M].bitcast(F32)
         nc.vector.tensor_tensor(half_s[:], h2[:].indirect(picks[:]), half_pw[:], ALU.mult)
         c0_pw = sb.tile([P, M], F32, name="c0_pw")
-        nc.vector.tensor_tensor(c0_pw[:], c0_ps[:], half_pw[:], ALU.mult)
-        xg0 = half_pw[:].bitcast(BF16)
+        nc.vector.tensor_tensor(c0_pw[:], c0_ps, half_pw[:], ALU.mult)
+        xg0 = sb.tile([P, J], BF16, name="xg0")[:]
         nc.vector.tensor_copy(xg0, x_tiles[0][:].indirect(slots[:]))
-        th = sb.tile([P, M], F32, name="th")
-        th_sq = sb.tile([P, M], F32, name="th_sq")
-        nc.scalar.activation(th[:], half_s[:], ACT.Tanh)
-        nc.scalar.activation(th_sq[:], th[:], ACT.Square)
         h1_sq = sb.tile([P, J], F32, name="h1_sq")
         nc.scalar.activation(h1_sq[:], h1[:], ACT.Square)
-        for e in range(4):
-            nc.tensor.transpose(js_ps[:, e, :], js_cols[:, e : e + 1].to_broadcast([P, P]), identity[:])
-        gain_js = sb.tile([P, J], F32, name="gain_js")
-        nc.scalar.activation(gain_js[:].rearrange("p (c e) -> p c e", e=4), js_ps[:].rearrange("p e c -> p c e"), ACT.Copy, scale=gain_col[:])
+        sech_sq = sb.tile([P, J], F32, name="sech_sq")
+        nc.scalar.activation(sech_sq[:], h1_sq[:], ACT.Identity, scale=-1.0, bias=1.0)
+        th, th_sq = h1_sq[:, 0:M], h1_sq[:, M:J]
+        nc.scalar.activation(th, half_s[:], ACT.Tanh)
+        nc.scalar.activation(th_sq, th, ACT.Square)
+        scaled = sb.tile([P, PACK, R], F32, name="scaled")
+        for t in range(PACK):
+            nc.tensor.transpose(js_ps[:, t, :], sech_sq[:, t:J:PACK], identity[:])
+        for t in range(PACK):
+            nc.scalar.activation(scaled[:, t, :], js_ps[:, t, :], ACT.Copy, scale=js_cols[:, t : t + 1])
+        for t in range(PACK):
+            nc.tensor.transpose(pw_ps[:, t, :], scaled[:, t, :], identity[:])
 
-        after_x0 = sb.tile([P, M + J], F32, name="after_x0", tag="x0", align_bytes=64)
-        bend, neg_all = after_x0[:, 0:M], after_x0[:, M : M + J]
-        nc.vector.scalar_tensor_tensor(bend[:], th_sq[:], 1.0, half_s[:], ALU.subtract, ALU.mult)
+        bend = sb.tile([P, M], F32, name="bend", tag="x0", align_bytes=64)
+        nc.vector.scalar_tensor_tensor(bend[:], th_sq, 1.0, half_s[:], ALU.subtract, ALU.mult)
         slope2 = sb.tile([P, M], F32, name="slope2")
-        nc.vector.scalar_tensor_tensor(slope2[:], th[:], 1.0, bend[:], ALU.add, ALU.subtract)
-        nc.vector.scalar_tensor_tensor(neg_all[:], h1_sq[:], 1.0, gain_js[:], ALU.subtract, ALU.mult)
+        nc.vector.scalar_tensor_tensor(slope2[:], th, 1.0, bend[:], ALU.add, ALU.subtract)
         nc.vector.tensor_tensor(s1[:].indirect(picks[:]), slope2[:], c0_pw[:], ALU.mult)
-        xg2 = c0_pw[:].bitcast(BF16)
-        nc.vector.tensor_copy(xg2, x_tiles[2][:].indirect(slots[:]))
-        gs = sb.tile([P, J], BF16, name="gs", tag="x2", align_bytes=64)
-        nc.vector.scalar_tensor_tensor(gs[:], s1[:], -1.0, neg_all[:], ALU.mult, ALU.mult)
+        gs = sb.tile([P, J], BF16, name="gs")
+        nc.vector.scalar_tensor_tensor(gs[:].rearrange("r (p t) -> r p t", t=PACK), s1[:].rearrange("r (p t) -> r p t", t=PACK), gain_col[:],
+                                       pw_ps[:].rearrange("r t p -> r p t"), ALU.mult, ALU.mult)
 
         out_rows = out.rearrange("(p b) r -> p b r", b=4)
-        xg = [xg0, sb.tile([P, J], BF16, name="xg1")[:], xg2, sb.tile([P, J], BF16, name="xg3", tag="s1")[:]]
-        x1_bf = sb.tile([P, T], BF16, name="x1_bf", tag="wo_raw", align_bytes=64)
+        xg = [xg0, sb.tile([P, J], BF16, name="xg1")[:], th.bitcast(BF16), slope2[:].bitcast(BF16)]
+        x1_bf = sb.tile([P, T], BF16, name="x1_bf")
         nc.scalar.activation(x1_bf[:], x_tiles[1][:], ACT.Copy)
         nc.scalar.activation(xg[1], x1_bf[:].indirect(slots[:]), ACT.Copy)
-        nc.vector.tensor_copy(xg[3], x_tiles[3][:].indirect(slots[:]))
+        for b in (2, 3):
+            nc.vector.tensor_copy(xg[b], x_tiles[b][:].indirect(slots[:]))
         early_in = sb.tile([P, 4 * J], BF16, name="early_in", align_bytes=64)
         last_in = sb.tile([P, J], BF16, name="last_in", tag="y0", align_bytes=64)
-        banks = [ps.tile([P, 2, P], F32, name=f"turned{n}", tag=f"bank{4 + n}") for n in range(4)]
-        turn(nc, early_in[:, 0:J], banks[0], xg[0], identity)
-        turn(nc, early_in[:, J : 2 * J], banks[1], xg[1], identity)
-        turn(nc, early_in[:, 2 * J : 3 * J], banks[1], xg[2], identity)
-        turn(nc, early_in[:, 3 * J : 4 * J], banks[2], gs[:], identity)
-        turn(nc, last_in[:], banks[3], xg[3], identity)
+        for n, (grouped, sources) in enumerate((
+            (early_in[:, 0:J], [xg[0]]),
+            (early_in[:, J : 3 * J], [xg[1], gs[:]]),
+            (early_in[:, 3 * J : 4 * J], [xg[2]]),
+            (last_in[:], [xg[3]]),
+        )):
+            bank = ps.tile([P, len(sources), 2, P], F32, name=f"turned{n}", tag=f"bank{4 + n}")
+            turn(nc, grouped, bank, sources, identity)
         early_codes, early_scales = quantize(nc, sb, early_in, "early", sb.tile([P, 4 * P], U32, name="early_codes", tag="x3", align_bytes=64))
         last_codes, last_scales = quantize(nc, sb, last_in, "last")
-        codes = [early_codes[:, b * P : (b + 1) * P] for b in range(3)] + [last_codes[:]]
-        scales = [early_scales[:, b * P : (b + 1) * P] for b in range(3)] + [last_scales[:]]
-        gt_codes, gt_scales = early_codes[:, 3 * P : 4 * P], early_scales[:, 3 * P : 4 * P]
+        codes = [early_codes[:, b * P : (b + 1) * P] for b in (0, 1, 3)] + [last_codes[:]]
+        scales = [early_scales[:, b * P : (b + 1) * P] for b in (0, 1, 3)] + [last_scales[:]]
+        gt_codes, gt_scales = early_codes[:, 2 * P : 3 * P], early_scales[:, 2 * P : 3 * P]
         for b0, b1, tag in ((0, 3, "bank2"), (3, 4, "bank3")):
             gw_ps = ps.tile([P, b1 - b0, R], F32, name=f"gw_ps{b0}", tag=tag)
             for b in range(b0, b1):

@@ -19,23 +19,46 @@ ALU = mybir.AluOpType
 
 P = 128
 PACK = 4
+GROUP = 16
 HALF = J // 2
+X_BLOCKS = K // P
+LINE = 4
+ALIGN = 64
 
 
 def interleaved_views(grouped, raw):
     return (
-        grouped[:].rearrange("p (c i t) -> p c t i", i=4, t=PACK),
-        raw[:].rearrange("p t (c i) -> p c t i", i=4),
+        grouped[:].rearrange("p (c i t) -> p c t i", i=LINE, t=PACK),
+        raw[:].rearrange("p t (c i) -> p c t i", i=LINE),
     )
 
 
-def quantize(nc, pool, grouped, name, codes=None):
-    width = grouped.shape[1] // PACK
-    if codes is None:
-        codes = pool.tile([P, width], U32, name=name + "_codes", align_bytes=64)
-    scales = pool.tile([P, width], U8, name=name + "_scales", align_bytes=64)
-    nc.vector.quantize_mx(out=codes[:].bitcast(FP8X4), scales=scales[:], in_=grouped[:])
+def mx_tiles(pool, width, name, codes_tag):
+    codes = pool.tile([P, width], U32, name=name + "_codes", tag=codes_tag, align_bytes=ALIGN)
+    scales = pool.tile([P, width], U8, name=name + "_scales", align_bytes=ALIGN)
     return codes, scales
+
+
+def quantize(nc, operand, grouped):
+    codes, scales = operand
+    nc.vector.quantize_mx(out=codes[:].bitcast(FP8X4), scales=scales[:], in_=grouped[:])
+
+
+def columns(operand, start, stop):
+    codes, scales = operand
+    return codes[:, start:stop], scales[:, start:stop]
+
+
+def product(nc, out, stationary, moving, moving_dtype):
+    nc.tensor.matmul_mx(
+        out=out,
+        lhsT=stationary[0].bitcast(FP8X4),
+        lhsT_scale=stationary[1],
+        rhs=moving[0].bitcast(moving_dtype),
+        rhs_scale=moving[1],
+        start=True,
+        stop=True,
+    )
 
 
 def turn(nc, grouped, bank, sources, identity):
@@ -55,11 +78,11 @@ def tile_attend_cpickact_w_kernel(tc, tab_words, tab_scales, w1, bias, gain, pw,
         sb = ctx.enter_context(tc.tile_pool(name="sb", bufs=1))
         ps = ctx.enter_context(tc.psum_pool(name="ps", bufs=1))
 
-        slots = sb.tile([P, J // 16], U16, name="slots")
+        slots = sb.tile([P, J // GROUP], U16, name="slots")
         nc.sync.dma_start(slots[:], offs)
-        picks = sb.tile([P, M // 16], U16, name="picks")
+        picks = sb.tile([P, M // GROUP], U16, name="picks")
         nc.sync.dma_start(picks[:], offs2)
-        tab_w = sb.tile([P, T], U16, name="tab_w", tag="tab_w", align_bytes=64)
+        tab_w = sb.tile([P, T], U16, name="tab_w", tag="tab_w", align_bytes=ALIGN)
         nc.sync.dma_start(tab_w[:].bitcast(I32), tab_words[0].bitcast(I32))
         tab_s = sb.tile([P, T], U8, name="tab_s")
         nc.vector.memset(tab_s[:, 0 : T // 2].bitcast(I32), 0)
@@ -70,7 +93,7 @@ def tile_attend_cpickact_w_kernel(tc, tab_words, tab_scales, w1, bias, gain, pw,
         identity = sb.tile([P, P], F32, name="identity")
         make_identity(nc, identity[:])
 
-        w1_raw = sb.tile([P, PACK, R], F32, name="w1_raw", tag="w1_raw", align_bytes=64)
+        w1_raw = sb.tile([P, PACK, R], F32, name="w1_raw", tag="w1_raw", align_bytes=ALIGN)
         nc.sync.dma_start(w1_raw[:], w1.rearrange("(p t) r -> p t r", t=PACK))
         pw_cols = sb.tile([P, 2], F32, name="pw_cols")
         nc.sync.dma_start(pw_cols[:], pw.rearrange("o (p e) -> (o p) e", e=2))
@@ -80,112 +103,131 @@ def tile_attend_cpickact_w_kernel(tc, tab_words, tab_scales, w1, bias, gain, pw,
         nc.sync.dma_start(bias_col[:], bias)
         gain_col = sb.tile([P, 1], F32, name="gain_col")
         nc.sync.dma_start(gain_col[:], gain)
-        js_cols = sb.tile([P, 4], F32, name="js_cols")
-        nc.sync.dma_start(js_cols[:], js.rearrange("o (p e) -> (o p) e", e=4))
+        js_cols = sb.tile([P, PACK], F32, name="js_cols")
+        nc.sync.dma_start(js_cols[:], js.rearrange("o (p t) -> (o p) t", t=PACK))
         dy_raw = sb.tile([P, PACK, M], F32, name="dy_raw")
         nc.sync.dma_start(dy_raw[:], dy.rearrange("(p t) m -> p t m", t=PACK))
-        x_rows = xrows.rearrange("(p b) t -> p b t", b=4)
-        x_tiles = [sb.tile([P, T], F32, name=f"x{b}", tag=f"x{b}", align_bytes=64) for b in range(4)]
-        for b in range(4):
+        x_rows = xrows.rearrange("(p b) t -> p b t", b=X_BLOCKS)
+        x_tiles = [sb.tile([P, T], F32, name=f"x{b}", tag=f"x{b}", align_bytes=ALIGN) for b in range(X_BLOCKS)]
+        for b in range(X_BLOCKS):
             nc.sync.dma_start(x_tiles[b][:], x_rows[:, b, :])
-        old_sb = sb.tile([P, 4, R], F32, name="old_sb")
-        nc.sync.dma_start(old_sb[:], old.rearrange("(p b) r -> p b r", b=4))
+        old_sb = sb.tile([P, X_BLOCKS, R], F32, name="old_sb")
+        nc.sync.dma_start(old_sb[:], old.rearrange("(p b) r -> p b r", b=X_BLOCKS))
 
         s1 = sb.tile([P, J], F32, name="s1")
         nc.vector.memset(s1[:], 0.0)
 
-        w1_grouped = sb.tile([P, R * PACK], BF16, name="w1_grouped", align_bytes=64)
+        w1_grouped = sb.tile([P, R * PACK], BF16, name="w1_grouped", align_bytes=ALIGN)
         nc.scalar.activation(*interleaved_views(w1_grouped, w1_raw), ACT.Copy)
-        w1_codes, w1_scales = quantize(nc, sb, w1_grouped, "w1")
-        js_ps = ps.tile([P, 4, P], F32, name="js_ps", tag="bank0")
-        pw_ps = ps.tile([P, 4, P], F32, name="pw_ps", tag="bank1")
-        a_ps = [bank[:, 0:2, :].rearrange("p e c -> p (e c)") for bank in (pw_ps, js_ps)]
-        for e in range(2):
-            nc.tensor.transpose(pw_ps[:, e, :], pw_cols[:, e : e + 1].to_broadcast([P, P]), identity[:])
-        half_pw = sb.tile([P, M], F32, name="half_pw")
-        nc.scalar.activation(half_pw[:].rearrange("p (c e) -> p c e", e=2), pw_ps[:, 0:2, :].rearrange("p e c -> p c e"), ACT.Copy, scale=0.5)
+        w1_mx = mx_tiles(sb, R, "w1", "w1_codes")
+        quantize(nc, w1_mx, w1_grouped)
 
-        tab_wg = [sb.tile([P, HALF], U16, name="tab_wg0", align_bytes=64), sb.tile([P, HALF], U16, name="tab_wg1", tag="w1_raw", align_bytes=64)]
-        tab_sg = sb.tile([P, J], U8, name="tab_sg", align_bytes=64)
+        bank_b = ps.tile([P, PACK, P], F32, name="bank_b")
+        bank_a = ps.tile([P, PACK, P], F32, name="bank_a")
+        a_ps = [bank[:, 0:2, :].rearrange("p e c -> p (e c)") for bank in (bank_a, bank_b)]
+
+        for e in range(2):
+            nc.tensor.transpose(bank_a[:, e, :], pw_cols[:, e : e + 1].to_broadcast([P, P]), identity[:])
+        half_pw = sb.tile([P, M], F32, name="half_pw")
+        nc.scalar.activation(
+            half_pw[:].rearrange("p (c e) -> p c e", e=2), bank_a[:, 0:2, :].rearrange("p e c -> p c e"), ACT.Copy, scale=0.5
+        )
+
+        tab_wg = [
+            sb.tile([P, HALF], U16, name="tab_wg0", align_bytes=ALIGN),
+            sb.tile([P, HALF], U16, name="tab_wg1", tag="w1_raw", align_bytes=ALIGN),
+        ]
+        tab_sg = sb.tile([P, J], U8, name="tab_sg", align_bytes=ALIGN)
         h1 = sb.tile([P, J], F32, name="h1")
         h2 = sb.tile([P, J], F32, name="h2")
         for h in range(2):
             cols = slice(h * HALF, (h + 1) * HALF)
-            part = slots[:, h * HALF // 16 : (h + 1) * HALF // 16]
-            nc.vector.tensor_copy(tab_wg[h][:], tab_w[:].indirect(part))
-            nc.vector.tensor_copy(tab_sg[:, cols], tab_s[:].indirect(part))
-            nc.tensor.matmul_mx(out=a_ps[h], lhsT=w1_codes[:].bitcast(FP8X4), lhsT_scale=w1_scales[:],
-                                rhs=tab_wg[h][:].bitcast(FP4X4), rhs_scale=tab_sg[:, cols], start=True, stop=True)
+            entries = slots[:, h * HALF // GROUP : (h + 1) * HALF // GROUP]
+            nc.vector.tensor_copy(tab_wg[h][:], tab_w[:].indirect(entries))
+            nc.vector.tensor_copy(tab_sg[:, cols], tab_s[:].indirect(entries))
+            product(nc, a_ps[h], columns(w1_mx, 0, R), (tab_wg[h][:], tab_sg[:, cols]), FP4X4)
             nc.scalar.activation(h1[:, cols], a_ps[h], ACT.Tanh, bias=bias_col[:])
             nc.scalar.activation(h2[:, cols], h1[:, cols], ACT.Copy, scale=gain_col[:])
 
-        wo_grouped = sb.tile([P, R * PACK], BF16, name="wo_grouped", align_bytes=64)
+        wo_grouped = sb.tile([P, R * PACK], BF16, name="wo_grouped", align_bytes=ALIGN)
         nc.scalar.activation(*interleaved_views(wo_grouped, wo_raw), ACT.Copy)
-        dy_grouped = sb.tile([P, M * PACK], BF16, name="dy_grouped", tag="tab_w", align_bytes=64)
+        dy_grouped = sb.tile([P, M * PACK], BF16, name="dy_grouped", tag="tab_w", align_bytes=ALIGN)
         nc.vector.tensor_copy(*interleaved_views(dy_grouped, dy_raw))
-        wo_codes, wo_scales = quantize(nc, sb, wo_grouped, "wo")
-        dy_codes, dy_scales = quantize(nc, sb, dy_grouped, "dy")
+        wo_mx = mx_tiles(sb, R, "wo", "wo_codes")
+        quantize(nc, wo_mx, wo_grouped)
+        dy_mx = mx_tiles(sb, M, "dy", "dy_codes")
+        quantize(nc, dy_mx, dy_grouped)
         c0_ps = a_ps[1]
-        nc.tensor.matmul_mx(out=c0_ps, lhsT=wo_codes[:].bitcast(FP8X4), lhsT_scale=wo_scales[:],
-                            rhs=dy_codes[:].bitcast(FP8X4), rhs_scale=dy_scales[:], start=True, stop=True)
+        product(nc, c0_ps, columns(wo_mx, 0, R), columns(dy_mx, 0, M), FP8X4)
 
-        half_s = dy_grouped[:, 0 : 2 * M].bitcast(F32)
-        nc.vector.tensor_tensor(half_s[:], h2[:].indirect(picks[:]), half_pw[:], ALU.mult)
-        c0_pw = sb.tile([P, M], F32, name="c0_pw")
-        nc.vector.tensor_tensor(c0_pw[:], c0_ps, half_pw[:], ALU.mult)
-        xg0 = sb.tile([P, J], BF16, name="xg0")[:]
-        nc.vector.tensor_copy(xg0, x_tiles[0][:].indirect(slots[:]))
+        half_s = dy_raw[:, 0, :]
+        nc.vector.tensor_tensor(half_s, h2[:].indirect(picks[:]), half_pw[:], ALU.mult)
+        xg0 = sb.tile([P, J], BF16, name="xg0")
+        nc.vector.tensor_copy(xg0[:], x_tiles[0][:].indirect(slots[:]))
+
         h1_sq = sb.tile([P, J], F32, name="h1_sq")
         nc.scalar.activation(h1_sq[:], h1[:], ACT.Square)
-        sech_sq = sb.tile([P, J], F32, name="sech_sq")
-        nc.scalar.activation(sech_sq[:], h1_sq[:], ACT.Identity, scale=-1.0, bias=1.0)
+        tanh_slope = sb.tile([P, J], F32, name="tanh_slope")
+        nc.scalar.activation(tanh_slope[:], h1_sq[:], ACT.Identity, scale=-1.0, bias=1.0)
         th, th_sq = h1_sq[:, 0:M], h1_sq[:, M:J]
-        nc.scalar.activation(th, half_s[:], ACT.Tanh)
+        nc.scalar.activation(th, half_s, ACT.Tanh)
         nc.scalar.activation(th_sq, th, ACT.Square)
-        scaled = sb.tile([P, PACK, R], F32, name="scaled")
+        slope_js = sb.tile([P, PACK, R], F32, name="slope_js")
         for t in range(PACK):
-            nc.tensor.transpose(js_ps[:, t, :], sech_sq[:, t:J:PACK], identity[:])
+            nc.tensor.transpose(bank_a[:, t, :], tanh_slope[:, t:J:PACK], identity[:])
         for t in range(PACK):
-            nc.scalar.activation(scaled[:, t, :], js_ps[:, t, :], ACT.Copy, scale=js_cols[:, t : t + 1])
-        for t in range(PACK):
-            nc.tensor.transpose(pw_ps[:, t, :], scaled[:, t, :], identity[:])
+            nc.scalar.activation(slope_js[:, t, :], bank_a[:, t, :], ACT.Copy, scale=js_cols[:, t : t + 1])
 
-        bend = sb.tile([P, M], F32, name="bend", tag="x0", align_bytes=64)
-        nc.vector.scalar_tensor_tensor(bend[:], th_sq, 1.0, half_s[:], ALU.subtract, ALU.mult)
-        slope2 = sb.tile([P, M], F32, name="slope2")
-        nc.vector.scalar_tensor_tensor(slope2[:], th, 1.0, bend[:], ALU.add, ALU.subtract)
-        nc.vector.tensor_tensor(s1[:].indirect(picks[:]), slope2[:], c0_pw[:], ALU.mult)
+        after_x0 = sb.tile([P, 2, M], F32, name="after_x0", tag="x0", align_bytes=ALIGN)
+        bend, c0_pw = after_x0[:, 0, :], after_x0[:, 1, :]
+        nc.vector.scalar_tensor_tensor(bend, th_sq, 1.0, half_s, ALU.subtract, ALU.mult)
+        nc.vector.tensor_tensor(c0_pw, c0_ps, half_pw[:], ALU.mult)
+        silu_slope2 = sb.tile([P, M], F32, name="silu_slope2")
+        nc.vector.scalar_tensor_tensor(silu_slope2[:], th, 1.0, bend, ALU.add, ALU.subtract)
+        nc.vector.tensor_tensor(s1[:].indirect(picks[:]), silu_slope2[:], c0_pw, ALU.mult)
+
+        for t in range(PACK):
+            nc.tensor.transpose(bank_b[:, t, :], slope_js[:, t, :], identity[:])
         gs = sb.tile([P, J], BF16, name="gs")
-        nc.vector.scalar_tensor_tensor(gs[:].rearrange("r (p t) -> r p t", t=PACK), s1[:].rearrange("r (p t) -> r p t", t=PACK), gain_col[:],
-                                       pw_ps[:].rearrange("r t p -> r p t"), ALU.mult, ALU.mult)
+        nc.vector.scalar_tensor_tensor(
+            gs[:].rearrange("r (p t) -> r p t", t=PACK),
+            s1[:].rearrange("r (p t) -> r p t", t=PACK),
+            gain_col[:],
+            bank_b[:].rearrange("r t p -> r p t"),
+            ALU.mult,
+            ALU.mult,
+        )
 
-        out_rows = out.rearrange("(p b) r -> p b r", b=4)
-        xg = [xg0, sb.tile([P, J], BF16, name="xg1")[:], th.bitcast(BF16), slope2[:].bitcast(BF16)]
         x1_bf = sb.tile([P, T], BF16, name="x1_bf")
         nc.scalar.activation(x1_bf[:], x_tiles[1][:], ACT.Copy)
-        nc.scalar.activation(xg[1], x1_bf[:].indirect(slots[:]), ACT.Copy)
-        for b in (2, 3):
-            nc.vector.tensor_copy(xg[b], x_tiles[b][:].indirect(slots[:]))
-        early_in = sb.tile([P, 4 * J], BF16, name="early_in", align_bytes=64)
-        last_in = sb.tile([P, J], BF16, name="last_in", tag="y0", align_bytes=64)
-        for n, (grouped, sources) in enumerate((
-            (early_in[:, 0:J], [xg[0]]),
-            (early_in[:, J : 3 * J], [xg[1], gs[:]]),
-            (early_in[:, 3 * J : 4 * J], [xg[2]]),
-            (last_in[:], [xg[3]]),
-        )):
-            bank = ps.tile([P, len(sources), 2, P], F32, name=f"turned{n}", tag=f"bank{4 + n}")
+        xg1 = sb.tile([P, J], BF16, name="xg1")
+        nc.scalar.activation(xg1[:], x1_bf[:].indirect(slots[:]), ACT.Copy)
+        xg2, xg3 = th.bitcast(BF16), silu_slope2[:].bitcast(BF16)
+        nc.vector.tensor_copy(xg2, x_tiles[2][:].indirect(slots[:]))
+        nc.vector.tensor_copy(xg3, x_tiles[3][:].indirect(slots[:]))
+
+        early_in = sb.tile([P, 4 * J], BF16, name="early_in", align_bytes=ALIGN)
+        last_in = sb.tile([P, J], BF16, name="last_in", tag="early_out", align_bytes=ALIGN)
+        turns = (
+            (early_in[:, 0 : 2 * J], [xg1[:], gs[:]]),
+            (early_in[:, 2 * J : 4 * J], [xg0[:], xg2]),
+            (last_in[:], [xg3]),
+        )
+        for n, (grouped, sources) in enumerate(turns):
+            bank = ps.tile([P, len(sources), 2, P], F32, name=f"turned{n}")
             turn(nc, grouped, bank, sources, identity)
-        early_codes, early_scales = quantize(nc, sb, early_in, "early", sb.tile([P, 4 * P], U32, name="early_codes", tag="x3", align_bytes=64))
-        last_codes, last_scales = quantize(nc, sb, last_in, "last")
-        codes = [early_codes[:, b * P : (b + 1) * P] for b in (0, 1, 3)] + [last_codes[:]]
-        scales = [early_scales[:, b * P : (b + 1) * P] for b in (0, 1, 3)] + [last_scales[:]]
-        gt_codes, gt_scales = early_codes[:, 2 * P : 3 * P], early_scales[:, 2 * P : 3 * P]
-        for b0, b1, tag in ((0, 3, "bank2"), (3, 4, "bank3")):
-            gw_ps = ps.tile([P, b1 - b0, R], F32, name=f"gw_ps{b0}", tag=tag)
-            for b in range(b0, b1):
-                nc.tensor.matmul_mx(out=gw_ps[:, b - b0, :], lhsT=codes[b].bitcast(FP8X4), lhsT_scale=scales[b],
-                                    rhs=gt_codes.bitcast(FP8X4), rhs_scale=gt_scales, start=True, stop=True)
-            y = sb.tile([P, b1 - b0, R], F32, name=f"y{b0}", tag=f"y{b0}", align_bytes=64)
-            nc.vector.tensor_tensor(y[:], gw_ps[:], old_sb[:, b0:b1, :], ALU.add)
-            nc.sync.dma_start(out_rows[:, b0:b1, :], y[:])
+        early_mx = mx_tiles(sb, 4 * P, "early", "x3")
+        quantize(nc, early_mx, early_in)
+        last_mx = mx_tiles(sb, P, "last", "last_codes")
+        quantize(nc, last_mx, last_in)
+        xt1_mx, gt1_mx, xt0_mx, xt2_mx = [columns(early_mx, n * P, (n + 1) * P) for n in range(4)]
+        xt_mx = [xt0_mx, xt1_mx, xt2_mx, columns(last_mx, 0, P)]
+
+        out_rows = out.rearrange("(p b) r -> p b r", b=X_BLOCKS)
+        for first, stop, tag in ((0, X_BLOCKS - 1, "early_out"), (X_BLOCKS - 1, X_BLOCKS, "last_out")):
+            gw_ps = ps.tile([P, stop - first, R], F32, name=f"gw_ps{first}")
+            for b in range(first, stop):
+                product(nc, gw_ps[:, b - first, :], xt_mx[b], gt1_mx, FP8X4)
+            y = sb.tile([P, stop - first, R], F32, name=f"y{first}", tag=tag, align_bytes=ALIGN)
+            nc.vector.tensor_tensor(y[:], gw_ps[:], old_sb[:, first:stop, :], ALU.add)
+            nc.sync.dma_start(out_rows[:, first:stop, :], y[:])

@@ -160,8 +160,10 @@ def tile_attend_cpickact_w_kernel(tc, tab_words, tab_scales, w1, bias, gain, pw,
         c0_ps = a_ps[1]
         product(nc, c0_ps, columns(wo_mx, 0, R), columns(dy_mx, 0, M), FP8X4)
 
-        half_s = dy_raw[:, 0, :]
+        half_s = dy_grouped[:, 0 : 2 * M].bitcast(F32)
         nc.vector.tensor_tensor(half_s, h2[:].indirect(picks[:]), half_pw[:], ALU.mult)
+        c0_pw = sb.tile([P, M], F32, name="c0_pw")
+        nc.vector.tensor_tensor(c0_pw[:], c0_ps, half_pw[:], ALU.mult)
         xg0 = sb.tile([P, J], BF16, name="xg0")
         nc.vector.tensor_copy(xg0[:], x_tiles[0][:].indirect(slots[:]))
 
@@ -174,26 +176,24 @@ def tile_attend_cpickact_w_kernel(tc, tab_words, tab_scales, w1, bias, gain, pw,
         nc.scalar.activation(th_sq, th, ACT.Square)
         slope_js = sb.tile([P, PACK, R], F32, name="slope_js")
         for t in range(PACK):
-            nc.tensor.transpose(bank_a[:, t, :], tanh_slope[:, t:J:PACK], identity[:])
+            nc.tensor.transpose(bank_b[:, t, :], tanh_slope[:, t:J:PACK], identity[:])
         for t in range(PACK):
-            nc.scalar.activation(slope_js[:, t, :], bank_a[:, t, :], ACT.Copy, scale=js_cols[:, t : t + 1])
+            nc.scalar.activation(slope_js[:, t, :], bank_b[:, t, :], ACT.Copy, scale=js_cols[:, t : t + 1])
+        for t in range(PACK):
+            nc.tensor.transpose(bank_a[:, t, :], slope_js[:, t, :], identity[:])
 
-        after_x0 = sb.tile([P, 2, M], F32, name="after_x0", tag="x0", align_bytes=ALIGN)
-        bend, c0_pw = after_x0[:, 0, :], after_x0[:, 1, :]
-        nc.vector.scalar_tensor_tensor(bend, th_sq, 1.0, half_s, ALU.subtract, ALU.mult)
-        nc.vector.tensor_tensor(c0_pw, c0_ps, half_pw[:], ALU.mult)
+        bend = sb.tile([P, M], F32, name="bend", tag="x0", align_bytes=ALIGN)
+        nc.vector.scalar_tensor_tensor(bend[:], th_sq, 1.0, half_s, ALU.subtract, ALU.mult)
         silu_slope2 = sb.tile([P, M], F32, name="silu_slope2")
-        nc.vector.scalar_tensor_tensor(silu_slope2[:], th, 1.0, bend, ALU.add, ALU.subtract)
-        nc.vector.tensor_tensor(s1[:].indirect(picks[:]), silu_slope2[:], c0_pw, ALU.mult)
+        nc.vector.scalar_tensor_tensor(silu_slope2[:], th, 1.0, bend[:], ALU.add, ALU.subtract)
+        nc.vector.tensor_tensor(s1[:].indirect(picks[:]), silu_slope2[:], c0_pw[:], ALU.mult)
 
-        for t in range(PACK):
-            nc.tensor.transpose(bank_b[:, t, :], slope_js[:, t, :], identity[:])
         gs = sb.tile([P, J], BF16, name="gs")
         nc.vector.scalar_tensor_tensor(
             gs[:].rearrange("r (p t) -> r p t", t=PACK),
             s1[:].rearrange("r (p t) -> r p t", t=PACK),
             gain_col[:],
-            bank_b[:].rearrange("r t p -> r p t"),
+            bank_a[:].rearrange("r t p -> r p t"),
             ALU.mult,
             ALU.mult,
         )
@@ -206,28 +206,32 @@ def tile_attend_cpickact_w_kernel(tc, tab_words, tab_scales, w1, bias, gain, pw,
         nc.vector.tensor_copy(xg2, x_tiles[2][:].indirect(slots[:]))
         nc.vector.tensor_copy(xg3, x_tiles[3][:].indirect(slots[:]))
 
-        early_in = sb.tile([P, 4 * J], BF16, name="early_in", align_bytes=ALIGN)
-        last_in = sb.tile([P, J], BF16, name="last_in", tag="early_out", align_bytes=ALIGN)
+        xt0_in = sb.tile([P, J], BF16, name="xt0_in", tag="x1", align_bytes=ALIGN)
+        xt1_gt1_in = sb.tile([P, 2 * J], BF16, name="xt1_gt1_in", align_bytes=ALIGN)
+        xt23_in = sb.tile([P, 2 * J], BF16, name="xt23_in", tag="first_out", align_bytes=ALIGN)
         turns = (
-            (early_in[:, 0 : 2 * J], [xg1[:], gs[:]]),
-            (early_in[:, 2 * J : 4 * J], [xg0[:], xg2]),
-            (last_in[:], [xg3]),
+            (xt0_in[:], [xg0[:]]),
+            (xt1_gt1_in[:], [xg1[:], gs[:]]),
+            (xt23_in[:, 0:J], [xg2]),
+            (xt23_in[:, J : 2 * J], [xg3]),
         )
         for n, (grouped, sources) in enumerate(turns):
             bank = ps.tile([P, len(sources), 2, P], F32, name=f"turned{n}")
             turn(nc, grouped, bank, sources, identity)
-        early_mx = mx_tiles(sb, 4 * P, "early", "x3")
-        quantize(nc, early_mx, early_in)
-        last_mx = mx_tiles(sb, P, "last", "last_codes")
-        quantize(nc, last_mx, last_in)
-        xt1_mx, gt1_mx, xt0_mx, xt2_mx = [columns(early_mx, n * P, (n + 1) * P) for n in range(4)]
-        xt_mx = [xt0_mx, xt1_mx, xt2_mx, columns(last_mx, 0, P)]
+
+        first_mx = mx_tiles(sb, 3 * P, "first", "x3")
+        quantize(nc, columns(first_mx, 0, P), xt0_in)
+        quantize(nc, columns(first_mx, P, 3 * P), xt1_gt1_in)
+        second_mx = mx_tiles(sb, 2 * P, "second", "second_codes")
+        quantize(nc, second_mx, xt23_in)
+        gt1_mx = columns(first_mx, 2 * P, 3 * P)
 
         out_rows = out.rearrange("(p b) r -> p b r", b=X_BLOCKS)
-        for first, stop, tag in ((0, X_BLOCKS - 1, "early_out"), (X_BLOCKS - 1, X_BLOCKS, "last_out")):
-            gw_ps = ps.tile([P, stop - first, R], F32, name=f"gw_ps{first}")
-            for b in range(first, stop):
-                product(nc, gw_ps[:, b - first, :], xt_mx[b], gt1_mx, FP8X4)
-            y = sb.tile([P, stop - first, R], F32, name=f"y{first}", tag=tag, align_bytes=ALIGN)
-            nc.vector.tensor_tensor(y[:], gw_ps[:], old_sb[:, first:stop, :], ALU.add)
-            nc.sync.dma_start(out_rows[:, first:stop, :], y[:])
+        for pair, (xt_mx, tag) in enumerate(((first_mx, "first_out"), (second_mx, "second_out"))):
+            blocks = slice(2 * pair, 2 * pair + 2)
+            gw_ps = ps.tile([P, 2, R], F32, name=f"gw_ps{pair}")
+            for n in range(2):
+                product(nc, gw_ps[:, n, :], columns(xt_mx, n * P, (n + 1) * P), gt1_mx, FP8X4)
+            y = sb.tile([P, 2, R], F32, name=f"y{pair}", tag=tag, align_bytes=ALIGN)
+            nc.vector.tensor_tensor(y[:], gw_ps[:], old_sb[:, blocks, :], ALU.add)
+            nc.sync.dma_start(out_rows[:, blocks, :], y[:])

from contextlib import ExitStack

import concourse.mybir as mybir
from concourse.masks import make_identity

K, R, F, T, J, M = 512, 128, 512, 2048, 512, 256
FLOPS = 2 * (K * R * J + F * R * M + J * K * R)

F32 = mybir.dt.float32
BF16 = mybir.dt.bfloat16
I32 = mybir.dt.int32
U32 = mybir.dt.uint32
U16 = mybir.dt.uint16
U8 = mybir.dt.uint8
FP8X4 = mybir.dt.float8_e4m3fn_x4
FP4X4 = mybir.dt.float4_e2m1fn_x4
ACT = mybir.ActivationFunctionType
ALU = mybir.AluOpType

P = 128
PACK = 4
GROUP = 16
HALF = J // 2
X_BLOCKS = K // P
LINE = 4
ALIGN = 64


def interleaved_views(grouped, raw):
    return (
        grouped[:].rearrange("p (c i t) -> p c t i", i=LINE, t=PACK),
        raw[:].rearrange("p t (c i) -> p c t i", i=LINE),
    )


def mx_tiles(pool, width, name, codes_tag):
    codes = pool.tile([P, width], U32, name=name + "_codes", tag=codes_tag, align_bytes=ALIGN)
    scales = pool.tile([P, width], U8, name=name + "_scales", align_bytes=ALIGN)
    return codes, scales


def quantize(nc, operand, grouped):
    codes, scales = operand
    nc.vector.quantize_mx(out=codes[:].bitcast(FP8X4), scales=scales[:], in_=grouped[:])


def columns(operand, start, stop):
    codes, scales = operand
    return codes[:, start:stop], scales[:, start:stop]


def product(nc, out, stationary, moving, moving_dtype):
    nc.tensor.matmul_mx(
        out=out,
        lhsT=stationary[0].bitcast(FP8X4),
        lhsT_scale=stationary[1],
        rhs=moving[0].bitcast(moving_dtype),
        rhs_scale=moving[1],
        start=True,
        stop=True,
    )


def turn(nc, grouped, bank, sources, identity):
    for n, rows in enumerate(sources):
        words = rows.bitcast(F32)
        for u in range(2):
            nc.tensor.transpose(bank[:, n, u, :], words[:, u : J // 2 : 2], identity[:])
    nc.scalar.copy(
        grouped.bitcast(F32).rearrange("p (n c u) -> p n c u", n=len(sources), u=2),
        bank[:].rearrange("p n u c -> p n c u"),
    )


def tile_attend_cpickact_w_kernel(tc, tab_words, tab_scales, w1, bias, gain, pw, wo, dy, js, xrows, old, offs, offs2, out):
    nc = tc.nc
    with ExitStack() as ctx:
        sb = ctx.enter_context(tc.tile_pool(name="sb", bufs=1))
        ps = ctx.enter_context(tc.psum_pool(name="ps", bufs=1))

        slots = sb.tile([P, J // GROUP], U16, name="slots")
        nc.sync.dma_start(slots[:], offs)
        picks = sb.tile([P, M // GROUP], U16, name="picks")
        nc.sync.dma_start(picks[:], offs2)
        tab_w = sb.tile([P, T], U16, name="tab_w", tag="tab_w", align_bytes=ALIGN)
        nc.sync.dma_start(tab_w[:].bitcast(I32), tab_words[0].bitcast(I32))
        tab_s = sb.tile([P, T], U8, name="tab_s")
        nc.vector.memset(tab_s[:, 0 : T // 2].bitcast(I32), 0)
        nc.gpsimd.memset(tab_s[:, T // 2 : T].bitcast(I32), 0)
        for q in range(4):
            nc.sync.dma_start(tab_s[32 * q : 32 * q + 4, :].bitcast(I32), tab_scales[0, 4 * q : 4 * q + 4, :].bitcast(I32))

        identity = sb.tile([P, P], F32, name="identity")
        make_identity(nc, identity[:])

        w1_raw = sb.tile([P, PACK, R], F32, name="w1_raw", tag="w1_raw", align_bytes=ALIGN)
        nc.sync.dma_start(w1_raw[:], w1.rearrange("(p t) r -> p t r", t=PACK))
        pw_cols = sb.tile([P, 2], F32, name="pw_cols")
        nc.sync.dma_start(pw_cols[:], pw.rearrange("o (p e) -> (o p) e", e=2))
        wo_raw = sb.tile([P, PACK, R], F32, name="wo_raw")
        nc.sync.dma_start(wo_raw[:], wo.rearrange("(p t) r -> p t r", t=PACK))
        bias_col = sb.tile([P, 1], F32, name="bias_col")
        nc.sync.dma_start(bias_col[:], bias)
        gain_col = sb.tile([P, 1], F32, name="gain_col")
        nc.sync.dma_start(gain_col[:], gain)
        js_cols = sb.tile([P, PACK], F32, name="js_cols")
        nc.sync.dma_start(js_cols[:], js.rearrange("o (p t) -> (o p) t", t=PACK))
        dy_raw = sb.tile([P, PACK, M], F32, name="dy_raw")
        nc.sync.dma_start(dy_raw[:], dy.rearrange("(p t) m -> p t m", t=PACK))
        x_rows = xrows.rearrange("(p b) t -> p b t", b=X_BLOCKS)
        x_tiles = [sb.tile([P, T], F32, name=f"x{b}", tag=f"x{b}", align_bytes=ALIGN) for b in range(X_BLOCKS)]
        for b in range(X_BLOCKS):
            nc.sync.dma_start(x_tiles[b][:], x_rows[:, b, :])
        old_sb = sb.tile([P, X_BLOCKS, R], F32, name="old_sb")
        nc.sync.dma_start(old_sb[:], old.rearrange("(p b) r -> p b r", b=X_BLOCKS))

        s1 = sb.tile([P, J], F32, name="s1")
        nc.vector.memset(s1[:], 0.0)

        w1_grouped = sb.tile([P, R * PACK], BF16, name="w1_grouped", align_bytes=ALIGN)
        nc.scalar.activation(*interleaved_views(w1_grouped, w1_raw), ACT.Copy)
        w1_mx = mx_tiles(sb, R, "w1", "w1_codes")
        quantize(nc, w1_mx, w1_grouped)

        bank_b = ps.tile([P, PACK, P], F32, name="bank_b")
        bank_a = ps.tile([P, PACK, P], F32, name="bank_a")
        a_ps = [bank[:, 0:2, :].rearrange("p e c -> p (e c)") for bank in (bank_a, bank_b)]

        for e in range(2):
            nc.tensor.transpose(bank_a[:, e, :], pw_cols[:, e : e + 1].to_broadcast([P, P]), identity[:])
        half_pw = sb.tile([P, M], F32, name="half_pw")
        nc.scalar.activation(
            half_pw[:].rearrange("p (c e) -> p c e", e=2), bank_a[:, 0:2, :].rearrange("p e c -> p c e"), ACT.Copy, scale=0.5
        )

        tab_wg = [
            sb.tile([P, HALF], U16, name="tab_wg0", align_bytes=ALIGN),
            sb.tile([P, HALF], U16, name="tab_wg1", tag="w1_raw", align_bytes=ALIGN),
        ]
        tab_sg = sb.tile([P, J], U8, name="tab_sg", align_bytes=ALIGN)
        h1 = sb.tile([P, J], F32, name="h1")
        h2 = sb.tile([P, J], F32, name="h2")
        for h in range(2):
            cols = slice(h * HALF, (h + 1) * HALF)
            entries = slots[:, h * HALF // GROUP : (h + 1) * HALF // GROUP]
            nc.vector.tensor_copy(tab_wg[h][:], tab_w[:].indirect(entries))
            nc.vector.tensor_copy(tab_sg[:, cols], tab_s[:].indirect(entries))
            product(nc, a_ps[h], columns(w1_mx, 0, R), (tab_wg[h][:], tab_sg[:, cols]), FP4X4)
            nc.scalar.activation(h1[:, cols], a_ps[h], ACT.Tanh, bias=bias_col[:])
            nc.scalar.activation(h2[:, cols], h1[:, cols], ACT.Copy, scale=gain_col[:])

        wo_grouped = sb.tile([P, R * PACK], BF16, name="wo_grouped", align_bytes=ALIGN)
        nc.scalar.activation(*interleaved_views(wo_grouped, wo_raw), ACT.Copy)
        dy_grouped = sb.tile([P, M * PACK], BF16, name="dy_grouped", tag="tab_w", align_bytes=ALIGN)
        nc.vector.tensor_copy(*interleaved_views(dy_grouped, dy_raw))
        wo_mx = mx_tiles(sb, R, "wo", "wo_codes")
        quantize(nc, wo_mx, wo_grouped)
        dy_mx = mx_tiles(sb, M, "dy", "dy_codes")
        quantize(nc, dy_mx, dy_grouped)
        c0_ps = a_ps[1]
        product(nc, c0_ps, columns(wo_mx, 0, R), columns(dy_mx, 0, M), FP8X4)

        half_s = dy_grouped[:, 0 : 2 * M].bitcast(F32)
        nc.vector.tensor_tensor(half_s, h2[:].indirect(picks[:]), half_pw[:], ALU.mult)
        c0_pw = sb.tile([P, M], F32, name="c0_pw")
        nc.vector.tensor_tensor(c0_pw[:], c0_ps, half_pw[:], ALU.mult)
        xg0 = sb.tile([P, J], BF16, name="xg0")
        nc.vector.tensor_copy(xg0[:], x_tiles[0][:].indirect(slots[:]))

        h1_sq = sb.tile([P, J], F32, name="h1_sq")
        nc.scalar.activation(h1_sq[:], h1[:], ACT.Square)
        tanh_slope = sb.tile([P, J], F32, name="tanh_slope")
        nc.scalar.activation(tanh_slope[:], h1_sq[:], ACT.Identity, scale=-1.0, bias=1.0)
        th, th_sq = h1_sq[:, 0:M], h1_sq[:, M:J]
        nc.scalar.activation(th, half_s, ACT.Tanh)
        nc.scalar.activation(th_sq, th, ACT.Square)
        slope_js = sb.tile([P, PACK, R], F32, name="slope_js")
        for t in range(PACK):
            nc.tensor.transpose(bank_b[:, t, :], tanh_slope[:, t:J:PACK], identity[:])
        for t in range(PACK):
            nc.scalar.activation(slope_js[:, t, :], bank_b[:, t, :], ACT.Copy, scale=js_cols[:, t : t + 1])
        for t in range(PACK):
            nc.tensor.transpose(bank_a[:, t, :], slope_js[:, t, :], identity[:])

        bend = sb.tile([P, M], F32, name="bend", tag="x0", align_bytes=ALIGN)
        nc.vector.scalar_tensor_tensor(bend[:], th_sq, 1.0, half_s, ALU.subtract, ALU.mult)
        silu_slope2 = sb.tile([P, M], F32, name="silu_slope2")
        nc.vector.scalar_tensor_tensor(silu_slope2[:], th, 1.0, bend[:], ALU.add, ALU.subtract)
        nc.vector.tensor_tensor(s1[:].indirect(picks[:]), silu_slope2[:], c0_pw[:], ALU.mult)

        gs = sb.tile([P, J], BF16, name="gs")
        nc.vector.scalar_tensor_tensor(
            gs[:].rearrange("r (p t) -> r p t", t=PACK),
            s1[:].rearrange("r (p t) -> r p t", t=PACK),
            gain_col[:],
            bank_a[:].rearrange("r t p -> r p t"),
            ALU.mult,
            ALU.mult,
        )

        x1_bf = sb.tile([P, T], BF16, name="x1_bf")
        nc.scalar.activation(x1_bf[:], x_tiles[1][:], ACT.Copy)
        xg1 = sb.tile([P, J], BF16, name="xg1")
        nc.scalar.activation(xg1[:], x1_bf[:].indirect(slots[:]), ACT.Copy)
        xg2, xg3 = th.bitcast(BF16), silu_slope2[:].bitcast(BF16)
        nc.vector.tensor_copy(xg2, x_tiles[2][:].indirect(slots[:]))
        nc.vector.tensor_copy(xg3, x_tiles[3][:].indirect(slots[:]))

        xt0_in = sb.tile([P, J], BF16, name="xt0_in", tag="x1", align_bytes=ALIGN)
        xt1_gt1_in = sb.tile([P, 2 * J], BF16, name="xt1_gt1_in", align_bytes=ALIGN)
        xt23_in = sb.tile([P, 2 * J], BF16, name="xt23_in", tag="first_out", align_bytes=ALIGN)
        turns = (
            (xt0_in[:], [xg0[:]]),
            (xt1_gt1_in[:], [xg1[:], gs[:]]),
            (xt23_in[:, 0:J], [xg2]),
            (xt23_in[:, J : 2 * J], [xg3]),
        )
        for n, (grouped, sources) in enumerate(turns):
            bank = ps.tile([P, len(sources), 2, P], F32, name=f"turned{n}")
            turn(nc, grouped, bank, sources, identity)

        first_mx = mx_tiles(sb, 3 * P, "first", "x3")
        quantize(nc, columns(first_mx, 0, P), xt0_in)
        quantize(nc, columns(first_mx, P, 3 * P), xt1_gt1_in)
        second_mx = mx_tiles(sb, 2 * P, "second", "second_codes")
        quantize(nc, second_mx, xt23_in)
        gt1_mx = columns(first_mx, 2 * P, 3 * P)

        out_rows = out.rearrange("(p b) r -> p b r", b=X_BLOCKS)
        for pair, (xt_mx, tag) in enumerate(((first_mx, "first_out"), (second_mx, "second_out"))):
            blocks = slice(2 * pair, 2 * pair + 2)
            gw_ps = ps.tile([P, 2, R], F32, name=f"gw_ps{pair}")
            for n in range(2):
                product(nc, gw_ps[:, n, :], columns(xt_mx, n * P, (n + 1) * P), gt1_mx, FP8X4)
            y = sb.tile([P, 2, R], F32, name=f"y{pair}", tag=tag, align_bytes=ALIGN)
            nc.vector.tensor_tensor(y[:], gw_ps[:], old_sb[:, blocks, :], ALU.add)
            nc.sync.dma_start(out_rows[:, blocks, :], y[:])
